import numpy as np
import ml_dtypes


def mxq(x, axis, fmt="e4m3"):
    dtype, down = {"e4m3": (ml_dtypes.float8_e4m3fn, 7), "e5m2": (ml_dtypes.float8_e5m2, 14)}[fmt]
    v = np.moveaxis(np.asarray(x, np.float32).astype(ml_dtypes.bfloat16).astype(np.float64), axis, -1)
    blocks = v.reshape(v.shape[:-1] + (-1, 32))
    amax = np.abs(blocks).max(-1, keepdims=True)
    byte = np.maximum(np.where(amax > 0, np.frexp(amax)[1] - 1 + 127, 0) - down, 1)
    scale = np.exp2(byte - 127.0)
    codes = (blocks / scale).astype(np.float32).astype(dtype).astype(np.float64)
    return np.moveaxis((codes * scale).reshape(v.shape), -1, axis)


WIDE = False


def mx_kscale(k, group=512):
    if not WIDE:
        return np.ones(k)
    levels = np.array([10, -10, 5, -5, 0])
    if group != 512:
        return np.exp2(np.random.permutation(np.resize(levels, k // group))).repeat(group)
    if k % 512:
        return np.exp2(np.random.permutation(np.resize(levels, k // 32))).repeat(32)
    a = np.empty((k // 512, 16))
    for p in range(k // 512):
        a[p, :8] = np.random.permutation(np.resize(levels, 8))
        for g in range(8):
            far = levels[np.abs(levels - a[p, g]) >= 10]
            a[p, g + 8] = far[np.random.randint(len(far))]
    return np.exp2(a.ravel()).repeat(32)


def f64(x):
    return np.asarray(x).astype(np.float64)


H, D, N = 4, 256, 1024


def setup_inputs():
    n = np.random.standard_normal
    s = mx_kscale(D, 0)
    u = mx_kscale(N)
    t = np.random.uniform(0.5, 2.0, N) * u
    v = n((H, N, 128))
    v[:, :, 127] = 1.0
    return {
        "q": n((H, D, N)).astype(np.float32),
        "qa": (np.random.uniform(0.5, 2.0, D) * s)[:, None].astype(np.float32),
        "ka": np.tile(np.random.uniform(0.5, 2.0, D) / s, (128, 1)).astype(np.float32),
        "k": n((H, N, D)).astype(np.float32),
        "t": t.reshape(N, 1).astype(np.float32),
        "v": (v / t[:, None]).astype(np.float32),
    }


def reference(q, qa, ka, k, t, v):
    fq = (np.where(f64(q) > 0, f64(q) + 1.0, np.exp(np.minimum(f64(q), 0.0)))) * f64(qa)
    fk = (np.where(f64(k) > 0, f64(k) + 1.0, np.exp(np.minimum(f64(k), 0.0)))) * f64(t) * f64(ka)[:1]
    S = (mxq(fk, 1, "e4m3").transpose(0, 2, 1) @ mxq(f64(v), 1, "e4m3")) / N
    y = mxq(fq, 1, "e4m3").transpose(0, 2, 1) @ mxq(S, 1, "e4m3")
    y = y / y[:, :, 127:128]
    return y

@@ -1,0 +1,369 @@
+from contextlib import ExitStack
+
+import concourse.mybir as mybir
+
+H, D, N, E = 4, 256, 1024, 128
+FLOPS = 2 * 2 * H * N * D * E
+
+F32 = mybir.dt.float32
+BF16 = mybir.dt.bfloat16
+U32 = mybir.dt.uint32
+U8 = mybir.dt.uint8
+FP8X4 = mybir.dt.float8_e4m3fn_x4
+ALU = mybir.AluOpType
+ACT = mybir.ActivationFunctionType
+
+P = 128
+PACK = 4
+ROWS = D // PACK
+PASS = P * PACK
+PASSES = N // PASS
+SLOT = 3 * ROWS
+Y_BANKS = 3
+QUERY_CHUNKS = [(0, 0, 512), (0, 512, 512), (1, 0, 512), (1, 512, 256), (1, 768, 128), (1, 896, 128)]
+
+
+def tile_rows_lin_elu1_norm_kernel(tc, q, qa, ka, k, t, v, out):
+    nc = tc.nc
+    with ExitStack() as ctx:
+        keep = ctx.enter_context(tc.tile_pool(name="keep", bufs=1))
+        work = ctx.enter_context(tc.tile_pool(name="work", bufs=2))
+        psum = ctx.enter_context(tc.psum_pool(name="psum", bufs=1))
+        ctx.enter_context(tc.manual_schedule())
+
+        key_units = [(pr, g, c) for pr in range(2) for g in range(PASSES) for c in range(2)]
+
+        zero = keep.tile([P, 8], F32, name="zero")
+        one = keep.tile([P, 8], F32, name="one")
+        t_sb = keep.tile([P, PASSES, PACK], F32, name="t_sb")
+        ka_sb = keep.tile([P, D], F32, name="ka_sb")
+        qa_sb = keep.tile([P, 8], F32, name="qa_sb")
+        qa_abs = keep.tile([P, 8], F32, name="qa_abs")
+        qa_step = keep.tile([P, 8], F32, name="qa_step")
+        qa_sign = keep.tile([P, 8], F32, name="qa_sign")
+        weight = [keep.tile([P, PACK, D], F32, name="weight%d" % g) for g in range(PASSES)]
+        k_raw = [keep.tile([P, PACK, D], F32, name="k_raw%d" % u) for u in range(len(key_units))]
+        v_raw = [keep.tile([P, PACK, E], F32, name="v_raw%d" % u) for u in range(len(key_units))]
+        q_raw = [keep.tile([P, PACK, w], F32, name="q_raw%d" % i) for i, (pr, n0, w) in enumerate(QUERY_CHUNKS)]
+        n_slots = 2 * PASSES * PACK
+        k_codes = keep.tile([P, n_slots + 1, 3, ROWS], U32, name="k_codes", align_bytes=64)
+        k_scales = keep.tile([P, n_slots + 1, 3, ROWS], U8, name="k_scales", align_bytes=64)
+        k_codes_flat = k_codes[:].rearrange("p s a m -> p (s a m)")
+        k_scales_flat = k_scales[:].rearrange("p s a m -> p (s a m)")
+        v_codes = [keep.tile([P, 2 * E], U32, name="v_codes%d" % s, align_bytes=64) for s in range(2 * PASSES)]
+        v_scales = [keep.tile([P, 2 * E], U8, name="v_scales%d" % s, align_bytes=64) for s in range(2 * PASSES)]
+        s_codes = [keep.tile([P, E], U32, name="s_codes%d" % pr, align_bytes=64) for pr in range(2)]
+        s_scales = [keep.tile([P, E], U8, name="s_scales%d" % pr, align_bytes=64) for pr in range(2)]
+        s_bank = [psum.tile([P, PACK, E], F32, name="s_bank%d" % pr) for pr in range(2)]
+        y_bank = [[psum.tile([P, 4, E], F32, name="y_bank%d_%d" % (c, b)) for b in range(Y_BANKS)] for c in range(2)]
+
+        def load_k(u, lo=0, hi=D):
+            pr, g, c = key_units[u]
+            src = k[2 * pr + c, g * PASS:(g + 1) * PASS, :].rearrange("(p j) d -> p j d", j=PACK)
+            nc.sync.dma_start(out=k_raw[u][:, :, lo:hi], in_=src[:, :, lo:hi])
+
+        def load_v(u):
+            pr, g, c = key_units[u]
+            nc.sync.dma_start(out=v_raw[u][:], in_=v[2 * pr + c, g * PASS:(g + 1) * PASS, :].rearrange("(p j) e -> p j e", j=PACK))
+
+        def load_q(i):
+            pr, n0, w = QUERY_CHUNKS[i]
+            src = q[2 * pr:2 * pr + 2].rearrange("c (p j) n -> (c p) j n", j=PACK)
+            nc.sync.dma_start(out=q_raw[i][:], in_=src[:, :, n0:n0 + w])
+
+        load_k(0, 0, D // 2)
+        nc.sync.dma_start(out=ka_sb[:], in_=ka)
+        nc.sync.dma_start(out=t_sb[:], in_=t.rearrange("(g p j) o -> p g (j o)", g=PASSES, j=PACK))
+        load_k(0, D // 2, D)
+        load_k(1)
+        for c in range(2):
+            nc.sync.dma_start(out=qa_sb[c * ROWS:(c + 1) * ROWS, 0:PACK], in_=qa.rearrange("(p j) o -> p (j o)", j=PACK))
+        load_k(2)
+        load_k(3)
+        load_v(0)
+        load_v(1)
+        load_v(2)
+        load_v(3)
+        load_k(4)
+        load_k(5)
+        load_v(4)
+        load_k(6)
+        load_v(5)
+        load_k(7)
+        load_v(6)
+        load_v(7)
+        load_q(0)
+        load_q(1)
+        load_q(2)
+        load_q(3)
+        load_q(4)
+        load_q(5)
+
+        nc.gpsimd.memset(zero[:], 0.0)
+        nc.scalar.activation(out=one[:], in_=zero[:], func=ACT.Exp)
+        nc.gpsimd.memset(k_codes[:, :, 0, :], 0)
+        nc.gpsimd.memset(k_scales[:, :, 0, :].bitcast(U32), 0)
+
+        k_exp, k_pos, k_bf = {}, {}, {}
+
+        def key_exp(u, lo=0, hi=D):
+            if u not in k_exp:
+                k_exp[u] = work.tile([P, PACK, D], F32, name="k_exp", tag="expo", bufs=4)
+            nc.scalar.activation(out=k_exp[u][:, :, lo:hi], in_=k_raw[u][:, :, lo:hi], func=ACT.Exp)
+
+        def key_relu(u, on_vector, lo=0, hi=D):
+            if u not in k_pos:
+                k_pos[u] = work.tile([P, PACK, D], F32, name="k_pos", tag="pos", bufs=4)
+            if on_vector:
+                nc.vector.tensor_scalar(out=k_pos[u][:, :, lo:hi], in0=k_raw[u][:, :, lo:hi], scalar1=0.0, scalar2=None, op0=ALU.max)
+            else:
+                nc.scalar.activation(out=k_pos[u][:, :, lo:hi], in_=k_raw[u][:, :, lo:hi], func=ACT.Relu)
+
+        def key_weight(g):
+            for j in range(PACK):
+                nc.vector.tensor_scalar(out=weight[g][:, j, :], in0=ka_sb[:], scalar1=t_sb[:, g, j:j + 1], scalar2=None, op0=ALU.mult)
+
+        def key_phi(u, lo=0, hi=D):
+            nc.vector.scalar_tensor_tensor(out=k_exp[u][:, :, lo:hi], in0=k_exp[u][:, :, lo:hi], scalar=one[:, 0:1],
+                                           in1=k_pos[u][:, :, lo:hi], op0=ALU.min, op1=ALU.add)
+
+        def key_round(u, lo=0, hi=D):
+            pr, g, c = key_units[u]
+            if (pr, g) not in k_bf:
+                k_bf[(pr, g)] = work.tile([P, PACK, 2, ROWS, PACK], BF16, name="k_bf", align_bytes=64)
+            dst = k_bf[(pr, g)][:, :, 1 - c, lo // PACK:hi // PACK, :].rearrange("p x m j -> p m j x")
+            nc.vector.tensor_tensor(out=dst, in0=k_exp[u][:, :, lo:hi].rearrange("p j (m x) -> p m j x", x=PACK),
+                                    in1=weight[g][:, :, lo:hi].rearrange("p j (m x) -> p m j x", x=PACK), op=ALU.mult)
+
+        def key_quant(pr, g):
+            for x in range(PACK):
+                c0 = ((pr * PASSES + g) * PACK + x) * SLOT + ROWS
+                nc.vector.quantize_mx(out=k_codes_flat[:, c0:c0 + 2 * ROWS].bitcast(FP8X4), scales=k_scales_flat[:, c0:c0 + 2 * ROWS],
+                                      in_=k_bf[(pr, g)][:, x].rearrange("p c m j -> p (c m j)"))
+
+        v_bf = {}
+
+        def value_round(u, on_vector):
+            pr, g, c = key_units[u]
+            if (pr, g) not in v_bf:
+                v_bf[(pr, g)] = work.tile([P, 2, E, PACK], BF16, name="v_bf", align_bytes=64)
+            dst = v_bf[(pr, g)][:, c].rearrange("p (b i) j -> p b j i", i=4)
+            src = v_raw[u][:].rearrange("p j (b i) -> p b j i", i=4)
+            if on_vector:
+                nc.vector.tensor_copy(out=dst, in_=src)
+            else:
+                nc.scalar.activation(out=dst, in_=src, func=ACT.Copy)
+
+        def value_quant(pr, g):
+            s = pr * PASSES + g
+            nc.vector.quantize_mx(out=v_codes[s][:].bitcast(FP8X4), scales=v_scales[s][:],
+                                  in_=v_bf[(pr, g)][:].rearrange("p c e j -> p (c e j)"))
+
+        def state_matmul(pr):
+            for x in range(PACK):
+                terms = [(g, c) for g in range(PASSES) for c in range(2)]
+                for i, (g, c) in enumerate(terms):
+                    c0 = ((pr * PASSES + g) * PACK + x) * SLOT + (1 - c) * 2 * ROWS
+                    s = pr * PASSES + g
+                    nc.tensor.matmul_mx(out=s_bank[pr][:, x, :], lhsT=k_codes_flat[:, c0:c0 + P].bitcast(FP8X4),
+                                        lhsT_scale=k_scales_flat[:, c0:c0 + P],
+                                        rhs=v_codes[s][:, c * E:(c + 1) * E].bitcast(FP8X4), rhs_scale=v_scales[s][:, c * E:(c + 1) * E],
+                                        start=(i == 0), stop=(i == len(terms) - 1))
+
+        s_bf = {}
+
+        def state_round(pr):
+            s_bf[pr] = work.tile([P, E, PACK], BF16, name="s_bf", align_bytes=64)
+            nc.vector.tensor_tensor(out=s_bf[pr][:], in0=s_bank[pr][:].rearrange("p x e -> p e x"),
+                                    in1=qa_sign[:, 0:PACK].unsqueeze(1).to_broadcast([P, E, PACK]), op=ALU.mult)
+
+        def state_quant(pr):
+            nc.vector.quantize_mx(out=s_codes[pr][:].bitcast(FP8X4), scales=s_scales[pr][:], in_=s_bf[pr][:].rearrange("p e x -> p (e x)"))
+
+        q_exp, q_pos, q_bf, q_codes, q_scales, inv, res = {}, {}, {}, {}, {}, {}, {}
+
+        def query_exp(i):
+            w = QUERY_CHUNKS[i][2]
+            q_exp[i] = work.tile([P, PACK, w], F32, name="q_exp", tag="expo", bufs=4)
+            nc.scalar.activation(out=q_exp[i][:], in_=q_raw[i][:], func=ACT.Exp)
+
+        def query_relu(i, on_vector):
+            w = QUERY_CHUNKS[i][2]
+            q_pos[i] = work.tile([P, PACK, w], F32, name="q_pos", tag="pos", bufs=4)
+            for j in range(PACK):
+                if on_vector:
+                    nc.vector.tensor_scalar(out=q_pos[i][:, j, :], in0=q_raw[i][:, j, :], scalar1=0.0, scalar2=qa_abs[:, j:j + 1],
+                                            op0=ALU.max, op1=ALU.mult)
+                else:
+                    nc.scalar.activation(out=q_pos[i][:, j, :], in_=q_raw[i][:, j, :], func=ACT.Relu, scale=qa_abs[:, j:j + 1])
+
+        def query_clip(i):
+            for j in range(PACK):
+                nc.vector.tensor_scalar(out=q_exp[i][:, j, :], in0=q_exp[i][:, j, :], scalar1=1.0, scalar2=qa_abs[:, j:j + 1],
+                                        op0=ALU.min, op1=ALU.mult)
+
+        def query_round(i):
+            w = QUERY_CHUNKS[i][2]
+            q_bf[i] = work.tile([P, w, PACK], BF16, name="q_bf", align_bytes=64)
+            nc.vector.tensor_tensor(out=q_bf[i][:].rearrange("p (b i) j -> p b j i", i=4),
+                                    in0=q_exp[i][:].rearrange("p j (b i) -> p b j i", i=4),
+                                    in1=q_pos[i][:].rearrange("p j (b i) -> p b j i", i=4), op=ALU.add)
+
+        def query_quant(i):
+            pr, n0, w = QUERY_CHUNKS[i]
+            q_codes[i] = work.tile([P, w], U32, name="q_codes", align_bytes=64)
+            q_scales[i] = work.tile([P, w], U8, name="q_scales", align_bytes=64)
+            nc.vector.quantize_mx(out=q_codes[i][:].bitcast(FP8X4), scales=q_scales[i][:], in_=q_bf[i][:].rearrange("p n j -> p (n j)"))
+
+        def query_matmul(i):
+            pr, n0, w = QUERY_CHUNKS[i]
+            for a in range(w // P):
+                for c in range(2):
+                    rows = slice(c * ROWS, (c + 1) * ROWS)
+                    nc.tensor.matmul_mx(out=y_bank[c][i % Y_BANKS][:, a, :], lhsT=q_codes[i][rows, a * P:(a + 1) * P].bitcast(FP8X4),
+                                        lhsT_scale=q_scales[i][rows, a * P:(a + 1) * P],
+                                        rhs=s_codes[pr][rows, :].bitcast(FP8X4), rhs_scale=s_scales[pr][rows, :],
+                                        start=True, stop=True)
+
+        def invert(i):
+            tiles = QUERY_CHUNKS[i][2] // P
+            for c in range(2):
+                inv[(i, c)] = work.tile([P, 8, 1], F32, name="inv", bufs=12)
+                nc.vector.reciprocal(out=inv[(i, c)][:, 0:tiles, :], in_=y_bank[c][i % Y_BANKS][:, 0:tiles, E - 1:E])
+
+        def finish(i, c, on_vector):
+            pr, n0, w = QUERY_CHUNKS[i]
+            tiles = w // P
+            bank = y_bank[c][i % Y_BANKS]
+            result = work.tile([P, tiles, E], F32, name="result", bufs=8)
+            if on_vector:
+                nc.vector.tensor_tensor(out=result[:], in0=bank[:, 0:tiles, :],
+                                        in1=inv[(i, c)][:, 0:tiles, :].to_broadcast([P, tiles, E]), op=ALU.mult)
+            else:
+                for a in range(tiles):
+                    nc.scalar.activation(out=result[:, a, :], in_=bank[:, a, :], func=ACT.Copy, scale=inv[(i, c)][:, a, :])
+            nc.sync.dma_start(out=out[2 * pr + c, n0:n0 + w, :].rearrange("(a r) e -> r a e", r=P), in_=result[:])
+
+        def query_weight_abs():
+            nc.vector.tensor_scalar(out=qa_step[:, 0:PACK], in0=qa_sb[:, 0:PACK], scalar1=0.0, scalar2=2.0 / N, op0=ALU.is_ge, op1=ALU.mult)
+            nc.vector.scalar_tensor_tensor(out=qa_abs[:, 0:PACK], in0=qa_sb[:, 0:PACK], scalar=-1.0, in1=qa_sb[:, 0:PACK], op0=ALU.mult, op1=ALU.max)
+
+        def query_weight_sign():
+            nc.vector.tensor_scalar(out=qa_sign[:, 0:PACK], in0=qa_step[:, 0:PACK], scalar1=-1.0 / N, scalar2=None, op0=ALU.add)
+
+        key_relu(0, True, 0, D // 2)
+        key_exp(0, 0, D // 2)
+        key_exp(0, D // 2, D)
+        key_relu(0, False, D // 2, D)
+        key_weight(0)
+        key_phi(0, 0, D // 2)
+        key_weight(1)
+        key_exp(1)
+        key_exp(2)
+        key_round(0, 0, D // 2)
+        key_relu(3, False)
+        key_phi(0, D // 2, D)
+        key_relu(1, True)
+        key_exp(3)
+        value_round(1, False)
+        key_relu(2, True)
+        key_phi(1)
+        key_phi(2)
+        value_round(3, False)
+        value_round(2, False)
+        key_exp(4)
+        key_round(1)
+        key_relu(4, False)
+        key_exp(5)
+        key_phi(3)
+        key_round(0, D // 2, D)
+        key_relu(6, False)
+        query_weight_abs()
+        key_relu(5, False)
+        key_round(2)
+        key_exp(6)
+        key_round(3)
+        key_phi(4)
+        key_quant(0, 0)
+        query_weight_sign()
+        key_quant(0, 1)
+        key_phi(5)
+        key_round(4)
+        key_phi(6)
+        value_round(0, False)
+        key_relu(7, False)
+        key_round(5)
+        query_exp(0)
+        key_round(6)
+        value_quant(0, 0)
+        value_quant(0, 1)
+        key_exp(7)
+        query_relu(0, False)
+        query_clip(0)
+        query_exp(1)
+        query_exp(3)
+        key_phi(7)
+        query_round(0)
+        query_relu(1, False)
+        query_exp(4)
+        state_matmul(0)
+        key_round(7)
+        key_quant(1, 0)
+        state_round(0)
+        value_round(5, False)
+        value_round(7, False)
+        query_clip(1)
+        query_quant(0)
+        value_round(4, False)
+        value_round(6, False)
+        query_exp(2)
+        state_quant(0)
+        query_round(1)
+        query_relu(2, False)
+        query_matmul(0)
+        query_relu(5, False)
+        query_clip(3)
+        invert(0)
+        key_quant(1, 1)
+        finish(0, 1, False)
+        value_quant(1, 1)
+        query_clip(2)
+        query_quant(1)
+        value_quant(1, 0)
+        state_matmul(1)
+        query_round(2)
+        state_round(1)
+        query_matmul(1)
+        query_exp(5)
+        invert(1)
+        query_quant(2)
+        query_relu(3, False)
+        state_quant(1)
+        query_matmul(2)
+        finish(0, 0, False)
+        finish(1, 1, False)
+        query_round(3)
+        invert(2)
+        query_clip(4)
+        finish(1, 0, False)
+        query_clip(5)
+        query_quant(3)
+        query_matmul(3)
+        query_round(5)
+        invert(3)
+        query_relu(4, False)
+        finish(2, 1, False)
+        query_round(4)
+        finish(2, 0, False)
+        query_quant(5)
+        finish(3, 1, False)
+        query_matmul(5)
+        query_quant(4)
+        query_matmul(4)
+        invert(5)
+        invert(4)
+        finish(3, 0, False)
+        finish(5, 1, False)
+        finish(5, 0, False)
+        finish(4, 1, True)
+        finish(4, 0, False)

@@ -15,12 +15,14 @@ ACT = mybir.ActivationFunctionType
 
 P = 128
 PACK = 4
+RUN = 4
 ROWS = D // PACK
-PASS = P * PACK
-PASSES = N // PASS
-SLOT = 3 * ROWS
+PASSES = N // (P * PACK)
+HALVES = D // P
 Y_BANKS = 3
-QUERY_CHUNKS = [(0, 0, 512), (0, 512, 512), (1, 0, 512), (1, 512, 256), (1, 768, 128), (1, 896, 128)]
+KEY_PIECES = [(0, 0, 1, 0, 128), (0, 0, 1, 128, 256), (0, 1, 2, 0, 256), (1, 0, 1, 0, 256), (1, 1, 2, 0, 256), (2, 0, 2, 0, 256), (3, 0, 2, 0, 256)]
+QUERY_CHUNKS = [(0, 0, 512), (0, 512, 512), (1, 0, 512), (1, 512, 256), (1, 768, 256)]
+QUERY_PARTS = [(0, 0, 512), (1, 0, 512), (2, 0, 512), (3, 0, 256), (4, 0, 128), (4, 128, 128)]
 
 
 def tile_rows_lin_elu1_norm_kernel(tc, q, qa, ka, k, t, v, out):
@@ -31,156 +33,162 @@ def tile_rows_lin_elu1_norm_kernel(tc, q, qa, ka, k, t, v, out):
         psum = ctx.enter_context(tc.psum_pool(name="psum", bufs=1))
         ctx.enter_context(tc.manual_schedule())
 
-        key_units = [(pr, g, c) for pr in range(2) for g in range(PASSES) for c in range(2)]
-
         zero = keep.tile([P, 8], F32, name="zero")
         one = keep.tile([P, 8], F32, name="one")
         t_sb = keep.tile([P, PASSES, PACK], F32, name="t_sb")
         ka_sb = keep.tile([P, D], F32, name="ka_sb")
         qa_sb = keep.tile([P, 8], F32, name="qa_sb")
         qa_abs = keep.tile([P, 8], F32, name="qa_abs")
+        qa_row = keep.tile([P, 8], F32, name="qa_row")
         qa_step = keep.tile([P, 8], F32, name="qa_step")
         qa_sign = keep.tile([P, 8], F32, name="qa_sign")
         weight = [keep.tile([P, PACK, D], F32, name="weight%d" % g) for g in range(PASSES)]
-        k_raw = [keep.tile([P, PACK, D], F32, name="k_raw%d" % u) for u in range(len(key_units))]
-        v_raw = [keep.tile([P, PACK, E], F32, name="v_raw%d" % u) for u in range(len(key_units))]
+        k_raw = [keep.tile([P, g1 - g0, PACK, hi - lo], F32, name="k_raw%d" % u) for u, (h, g0, g1, lo, hi) in enumerate(KEY_PIECES)]
+        v_raw = [keep.tile([P, PASSES, PACK, E], F32, name="v_raw%d" % h) for h in range(H)]
         q_raw = [keep.tile([P, PACK, w], F32, name="q_raw%d" % i) for i, (pr, n0, w) in enumerate(QUERY_CHUNKS)]
-        n_slots = 2 * PASSES * PACK
-        k_codes = keep.tile([P, n_slots + 1, 3, ROWS], U32, name="k_codes", align_bytes=64)
-        k_scales = keep.tile([P, n_slots + 1, 3, ROWS], U8, name="k_scales", align_bytes=64)
-        k_codes_flat = k_codes[:].rearrange("p s a m -> p (s a m)")
-        k_scales_flat = k_scales[:].rearrange("p s a m -> p (s a m)")
-        v_codes = [keep.tile([P, 2 * E], U32, name="v_codes%d" % s, align_bytes=64) for s in range(2 * PASSES)]
-        v_scales = [keep.tile([P, 2 * E], U8, name="v_scales%d" % s, align_bytes=64) for s in range(2 * PASSES)]
+        k_codes = [keep.tile([P, PASSES * D], U32, name="k_codes%d" % h, align_bytes=64) for h in range(H)]
+        k_scales = [keep.tile([P, PASSES * D], U8, name="k_scales%d" % h, align_bytes=64) for h in range(H)]
+        v_codes = [keep.tile([P, PASSES * E], U32, name="v_codes%d" % h, align_bytes=64) for h in range(H)]
+        v_scales = [keep.tile([P, PASSES * E], U8, name="v_scales%d" % h, align_bytes=64) for h in range(H)]
         s_codes = [keep.tile([P, E], U32, name="s_codes%d" % pr, align_bytes=64) for pr in range(2)]
         s_scales = [keep.tile([P, E], U8, name="s_scales%d" % pr, align_bytes=64) for pr in range(2)]
-        s_bank = [psum.tile([P, PACK, E], F32, name="s_bank%d" % pr) for pr in range(2)]
+        s_bank = [psum.tile([P, 2 * HALVES, E], F32, name="s_bank%d" % pr) for pr in range(2)]
         y_bank = [[psum.tile([P, 4, E], F32, name="y_bank%d_%d" % (c, b)) for b in range(Y_BANKS)] for c in range(2)]
 
-        def load_k(u, lo=0, hi=D):
-            pr, g, c = key_units[u]
-            src = k[2 * pr + c, g * PASS:(g + 1) * PASS, :].rearrange("(p j) d -> p j d", j=PACK)
-            nc.sync.dma_start(out=k_raw[u][:, :, lo:hi], in_=src[:, :, lo:hi])
+        def load_k(u):
+            h, g0, g1, lo, hi = KEY_PIECES[u]
+            src = k[h].rearrange("(g p j) d -> p g j d", g=PASSES, j=PACK)
+            if g1 - g0 == 1:
+                nc.sync.dma_start(out=k_raw[u][:, 0], in_=src[:, g0, :, lo:hi])
+            else:
+                nc.sync.dma_start(out=k_raw[u][:].rearrange("p g j d -> p g (j d)"), in_=src.rearrange("p g j d -> p g (j d)"))
 
-        def load_v(u):
-            pr, g, c = key_units[u]
-            nc.sync.dma_start(out=v_raw[u][:], in_=v[2 * pr + c, g * PASS:(g + 1) * PASS, :].rearrange("(p j) e -> p j e", j=PACK))
+        def load_v(h):
+            nc.sync.dma_start(out=v_raw[h][:].rearrange("p g j e -> p g (j e)"),
+                              in_=v[h].rearrange("(g p j) e -> p g (j e)", g=PASSES, j=PACK))
 
         def load_q(i):
             pr, n0, w = QUERY_CHUNKS[i]
             src = q[2 * pr:2 * pr + 2].rearrange("c (p j) n -> (c p) j n", j=PACK)
             nc.sync.dma_start(out=q_raw[i][:], in_=src[:, :, n0:n0 + w])
 
-        load_k(0, 0, D // 2)
+        load_k(0)
         nc.sync.dma_start(out=ka_sb[:], in_=ka)
         nc.sync.dma_start(out=t_sb[:], in_=t.rearrange("(g p j) o -> p g (j o)", g=PASSES, j=PACK))
-        load_k(0, D // 2, D)
         load_k(1)
-        for c in range(2):
-            nc.sync.dma_start(out=qa_sb[c * ROWS:(c + 1) * ROWS, 0:PACK], in_=qa.rearrange("(p j) o -> p (j o)", j=PACK))
         load_k(2)
         load_k(3)
+        load_k(4)
         load_v(0)
+        load_k(5)
         load_v(1)
+        for c in range(2):
+            nc.sync.dma_start(out=qa_sb[c * ROWS:(c + 1) * ROWS, 0:PACK], in_=qa.rearrange("(p j) o -> p (j o)", j=PACK))
+        with nc.allow_non_contiguous_dma(reason="one weight a partition"):
+            nc.sync.dma_start(out=qa_row[:, 0:HALVES], in_=qa.rearrange("(u r) o -> r (u o)", r=P))
+        load_k(6)
         load_v(2)
         load_v(3)
-        load_k(4)
-        load_k(5)
-        load_v(4)
-        load_k(6)
-        load_v(5)
-        load_k(7)
-        load_v(6)
-        load_v(7)
         load_q(0)
         load_q(1)
         load_q(2)
         load_q(3)
         load_q(4)
-        load_q(5)
 
         nc.gpsimd.memset(zero[:], 0.0)
         nc.scalar.activation(out=one[:], in_=zero[:], func=ACT.Exp)
-        nc.gpsimd.memset(k_codes[:, :, 0, :], 0)
-        nc.gpsimd.memset(k_scales[:, :, 0, :].bitcast(U32), 0)
 
-        k_exp, k_pos, k_bf = {}, {}, {}
+        k_exp, k_pos, k_bf, v_bf = {}, {}, {}, {}
 
-        def key_exp(u, lo=0, hi=D):
-            if u not in k_exp:
-                k_exp[u] = work.tile([P, PACK, D], F32, name="k_exp", tag="expo", bufs=4)
-            nc.scalar.activation(out=k_exp[u][:, :, lo:hi], in_=k_raw[u][:, :, lo:hi], func=ACT.Exp)
+        def key_exp(u):
+            k_exp[u] = work.tile(k_raw[u].shape, F32, name="k_exp", tag="expo", bufs=4)
+            nc.scalar.activation(out=k_exp[u][:], in_=k_raw[u][:], func=ACT.Exp)
 
-        def key_relu(u, on_vector, lo=0, hi=D):
-            if u not in k_pos:
-                k_pos[u] = work.tile([P, PACK, D], F32, name="k_pos", tag="pos", bufs=4)
+        def key_relu(u, on_vector):
+            k_pos[u] = work.tile(k_raw[u].shape, F32, name="k_pos", tag="pos", bufs=4)
             if on_vector:
-                nc.vector.tensor_scalar(out=k_pos[u][:, :, lo:hi], in0=k_raw[u][:, :, lo:hi], scalar1=0.0, scalar2=None, op0=ALU.max)
+                nc.vector.tensor_scalar(out=k_pos[u][:], in0=k_raw[u][:], scalar1=0.0, scalar2=None, op0=ALU.max)
             else:
-                nc.scalar.activation(out=k_pos[u][:, :, lo:hi], in_=k_raw[u][:, :, lo:hi], func=ACT.Relu)
+                nc.scalar.activation(out=k_pos[u][:], in_=k_raw[u][:], func=ACT.Relu)
 
-        def key_weight(g):
+        def key_weight(g, on_vector):
             for j in range(PACK):
-                nc.vector.tensor_scalar(out=weight[g][:, j, :], in0=ka_sb[:], scalar1=t_sb[:, g, j:j + 1], scalar2=None, op0=ALU.mult)
+                if on_vector:
+                    nc.vector.tensor_scalar(out=weight[g][:, j, :], in0=ka_sb[:], scalar1=t_sb[:, g, j:j + 1], scalar2=None, op0=ALU.mult)
+                else:
+                    nc.scalar.activation(out=weight[g][:, j, :], in_=ka_sb[:], func=ACT.Copy, scale=t_sb[:, g, j:j + 1])
 
-        def key_phi(u, lo=0, hi=D):
-            nc.vector.scalar_tensor_tensor(out=k_exp[u][:, :, lo:hi], in0=k_exp[u][:, :, lo:hi], scalar=one[:, 0:1],
-                                           in1=k_pos[u][:, :, lo:hi], op0=ALU.min, op1=ALU.add)
+        def key_phi(u):
+            nc.vector.scalar_tensor_tensor(out=k_exp[u][:], in0=k_exp[u][:], scalar=one[:, 0:1], in1=k_pos[u][:], op0=ALU.min, op1=ALU.add)
 
-        def key_round(u, lo=0, hi=D):
-            pr, g, c = key_units[u]
-            if (pr, g) not in k_bf:
-                k_bf[(pr, g)] = work.tile([P, PACK, 2, ROWS, PACK], BF16, name="k_bf", align_bytes=64)
-            dst = k_bf[(pr, g)][:, :, 1 - c, lo // PACK:hi // PACK, :].rearrange("p x m j -> p m j x")
-            nc.vector.tensor_tensor(out=dst, in0=k_exp[u][:, :, lo:hi].rearrange("p j (m x) -> p m j x", x=PACK),
-                                    in1=weight[g][:, :, lo:hi].rearrange("p j (m x) -> p m j x", x=PACK), op=ALU.mult)
+        def key_round(u):
+            h, g0, g1, lo, hi = KEY_PIECES[u]
+            if h not in k_bf:
+                k_bf[h] = work.tile([P, PASSES, D, PACK], BF16, name="k_bf", align_bytes=64)
+            for g in range(g0, g1):
+                nc.vector.tensor_tensor(out=k_bf[h][:, g, lo:hi, :].rearrange("p (b i) j -> p b j i", i=RUN),
+                                        in0=k_exp[u][:, g - g0].rearrange("p j (b i) -> p b j i", i=RUN),
+                                        in1=weight[g][:, :, lo:hi].rearrange("p j (b i) -> p b j i", i=RUN), op=ALU.mult)
 
-        def key_quant(pr, g):
-            for x in range(PACK):
-                c0 = ((pr * PASSES + g) * PACK + x) * SLOT + ROWS
-                nc.vector.quantize_mx(out=k_codes_flat[:, c0:c0 + 2 * ROWS].bitcast(FP8X4), scales=k_scales_flat[:, c0:c0 + 2 * ROWS],
-                                      in_=k_bf[(pr, g)][:, x].rearrange("p c m j -> p (c m j)"))
+        def key_quant(h):
+            nc.vector.quantize_mx(out=k_codes[h][:].bitcast(FP8X4), scales=k_scales[h][:], in_=k_bf[h][:].rearrange("p g d j -> p (g d j)"))
 
-        v_bf = {}
+        def value_round(h, on_vector):
+            v_bf[h] = work.tile([P, PASSES, E, PACK], BF16, name="v_bf", align_bytes=64)
+            for g in range(PASSES):
+                dst = v_bf[h][:, g].rearrange("p (b i) j -> p b j i", i=RUN)
+                src = v_raw[h][:, g].rearrange("p j (b i) -> p b j i", i=RUN)
+                if on_vector:
+                    nc.vector.tensor_copy(out=dst, in_=src)
+                else:
+                    nc.scalar.activation(out=dst, in_=src, func=ACT.Copy)
 
-        def value_round(u, on_vector):
-            pr, g, c = key_units[u]
-            if (pr, g) not in v_bf:
-                v_bf[(pr, g)] = work.tile([P, 2, E, PACK], BF16, name="v_bf", align_bytes=64)
-            dst = v_bf[(pr, g)][:, c].rearrange("p (b i) j -> p b j i", i=4)
-            src = v_raw[u][:].rearrange("p j (b i) -> p b j i", i=4)
+        def value_quant(h):
+            nc.vector.quantize_mx(out=v_codes[h][:].bitcast(FP8X4), scales=v_scales[h][:], in_=v_bf[h][:].rearrange("p g e j -> p (g e j)"))
+
+        def state_matmul(h):
+            for u in range(HALVES):
+                for g in range(PASSES):
+                    cols = slice(g * D + u * P, g * D + (u + 1) * P)
+                    nc.tensor.matmul_mx(out=s_bank[h // 2][:, (h % 2) * HALVES + u, :], lhsT=k_codes[h][:, cols].bitcast(FP8X4),
+                                        lhsT_scale=k_scales[h][:, cols],
+                                        rhs=v_codes[h][:, g * E:(g + 1) * E].bitcast(FP8X4), rhs_scale=v_scales[h][:, g * E:(g + 1) * E],
+                                        start=(g == 0), stop=(g == PASSES - 1))
+
+        s_out, s_in, s_bf = {}, {}, {}
+
+        def parked(pr):
+            return out[H - 1, pr * 2 * D:(pr + 1) * 2 * D, :]
+
+        def state_evict(pr, on_vector):
+            s_out[pr] = work.tile([P, 2 * HALVES, E], F32, name="s_out")
+            for a in range(2 * HALVES):
+                sign = qa_sign[:, a % HALVES:a % HALVES + 1]
+                if on_vector:
+                    nc.vector.tensor_scalar(out=s_out[pr][:, a, :], in0=s_bank[pr][:, a, :], scalar1=sign, scalar2=None, op0=ALU.mult)
+                else:
+                    nc.scalar.activation(out=s_out[pr][:, a, :], in_=s_bank[pr][:, a, :], func=ACT.Copy, scale=sign)
+
+        def state_park(pr):
+            nc.sync.dma_start(out=parked(pr).rearrange("(a r) e -> r a e", r=P), in_=s_out[pr][:])
+
+        def state_fetch(pr):
+            s_in[pr] = work.tile([P, PACK, E], F32, name="s_in")
+            nc.sync.dma_start(out=s_in[pr][:], in_=parked(pr).rearrange("(p x) e -> p x e", x=PACK))
+
+        def state_round(pr, on_vector):
+            s_bf[pr] = work.tile([P, E, PACK], BF16, name="s_bf", align_bytes=64)
+            dst = s_bf[pr][:].rearrange("p (b i) x -> p b x i", i=RUN)
+            src = s_in[pr][:].rearrange("p x (b i) -> p b x i", i=RUN)
             if on_vector:
                 nc.vector.tensor_copy(out=dst, in_=src)
             else:
                 nc.scalar.activation(out=dst, in_=src, func=ACT.Copy)
 
-        def value_quant(pr, g):
-            s = pr * PASSES + g
-            nc.vector.quantize_mx(out=v_codes[s][:].bitcast(FP8X4), scales=v_scales[s][:],
-                                  in_=v_bf[(pr, g)][:].rearrange("p c e j -> p (c e j)"))
-
-        def state_matmul(pr):
-            for x in range(PACK):
-                terms = [(g, c) for g in range(PASSES) for c in range(2)]
-                for i, (g, c) in enumerate(terms):
-                    c0 = ((pr * PASSES + g) * PACK + x) * SLOT + (1 - c) * 2 * ROWS
-                    s = pr * PASSES + g
-                    nc.tensor.matmul_mx(out=s_bank[pr][:, x, :], lhsT=k_codes_flat[:, c0:c0 + P].bitcast(FP8X4),
-                                        lhsT_scale=k_scales_flat[:, c0:c0 + P],
-                                        rhs=v_codes[s][:, c * E:(c + 1) * E].bitcast(FP8X4), rhs_scale=v_scales[s][:, c * E:(c + 1) * E],
-                                        start=(i == 0), stop=(i == len(terms) - 1))
-
-        s_bf = {}
-
-        def state_round(pr):
-            s_bf[pr] = work.tile([P, E, PACK], BF16, name="s_bf", align_bytes=64)
-            nc.vector.tensor_tensor(out=s_bf[pr][:], in0=s_bank[pr][:].rearrange("p x e -> p e x"),
-                                    in1=qa_sign[:, 0:PACK].unsqueeze(1).to_broadcast([P, E, PACK]), op=ALU.mult)
-
         def state_quant(pr):
             nc.vector.quantize_mx(out=s_codes[pr][:].bitcast(FP8X4), scales=s_scales[pr][:], in_=s_bf[pr][:].rearrange("p e x -> p (e x)"))
 
-        q_exp, q_pos, q_bf, q_codes, q_scales, inv, res = {}, {}, {}, {}, {}, {}, {}
+        q_exp, q_pos, q_bf, q_codes, q_scales, inv = {}, {}, {}, {}, {}, {}
 
         def query_exp(i):
             w = QUERY_CHUNKS[i][2]
@@ -202,168 +210,163 @@ def tile_rows_lin_elu1_norm_kernel(tc, q, qa, ka, k, t, v, out):
                 nc.vector.tensor_scalar(out=q_exp[i][:, j, :], in0=q_exp[i][:, j, :], scalar1=1.0, scalar2=qa_abs[:, j:j + 1],
                                         op0=ALU.min, op1=ALU.mult)
 
-        def query_round(i):
-            w = QUERY_CHUNKS[i][2]
-            q_bf[i] = work.tile([P, w, PACK], BF16, name="q_bf", align_bytes=64)
-            nc.vector.tensor_tensor(out=q_bf[i][:].rearrange("p (b i) j -> p b j i", i=4),
-                                    in0=q_exp[i][:].rearrange("p j (b i) -> p b j i", i=4),
-                                    in1=q_pos[i][:].rearrange("p j (b i) -> p b j i", i=4), op=ALU.add)
+        def query_round(s):
+            i, m0, w = QUERY_PARTS[s]
+            q_bf[s] = work.tile([P, w, PACK], BF16, name="q_bf", align_bytes=64)
+            nc.vector.tensor_tensor(out=q_bf[s][:].rearrange("p (b i) j -> p b j i", i=RUN),
+                                    in0=q_exp[i][:, :, m0:m0 + w].rearrange("p j (b i) -> p b j i", i=RUN),
+                                    in1=q_pos[i][:, :, m0:m0 + w].rearrange("p j (b i) -> p b j i", i=RUN), op=ALU.add)
 
-        def query_quant(i):
-            pr, n0, w = QUERY_CHUNKS[i]
-            q_codes[i] = work.tile([P, w], U32, name="q_codes", align_bytes=64)
-            q_scales[i] = work.tile([P, w], U8, name="q_scales", align_bytes=64)
-            nc.vector.quantize_mx(out=q_codes[i][:].bitcast(FP8X4), scales=q_scales[i][:], in_=q_bf[i][:].rearrange("p n j -> p (n j)"))
+        def query_quant(s):
+            w = QUERY_PARTS[s][2]
+            q_codes[s] = work.tile([P, w], U32, name="q_codes", align_bytes=64)
+            q_scales[s] = work.tile([P, w], U8, name="q_scales", align_bytes=64)
+            nc.vector.quantize_mx(out=q_codes[s][:].bitcast(FP8X4), scales=q_scales[s][:], in_=q_bf[s][:].rearrange("p n j -> p (n j)"))
 
-        def query_matmul(i):
-            pr, n0, w = QUERY_CHUNKS[i]
+        def query_matmul(s):
+            i, m0, w = QUERY_PARTS[s]
+            pr = QUERY_CHUNKS[i][0]
             for a in range(w // P):
                 for c in range(2):
                     rows = slice(c * ROWS, (c + 1) * ROWS)
-                    nc.tensor.matmul_mx(out=y_bank[c][i % Y_BANKS][:, a, :], lhsT=q_codes[i][rows, a * P:(a + 1) * P].bitcast(FP8X4),
-                                        lhsT_scale=q_scales[i][rows, a * P:(a + 1) * P],
+                    nc.tensor.matmul_mx(out=y_bank[c][s % Y_BANKS][:, a, :], lhsT=q_codes[s][rows, a * P:(a + 1) * P].bitcast(FP8X4),
+                                        lhsT_scale=q_scales[s][rows, a * P:(a + 1) * P],
                                         rhs=s_codes[pr][rows, :].bitcast(FP8X4), rhs_scale=s_scales[pr][rows, :],
                                         start=True, stop=True)
 
-        def invert(i):
-            tiles = QUERY_CHUNKS[i][2] // P
+        def invert(s):
+            tiles = QUERY_PARTS[s][2] // P
             for c in range(2):
-                inv[(i, c)] = work.tile([P, 8, 1], F32, name="inv", bufs=12)
-                nc.vector.reciprocal(out=inv[(i, c)][:, 0:tiles, :], in_=y_bank[c][i % Y_BANKS][:, 0:tiles, E - 1:E])
+                inv[(s, c)] = work.tile([P, 8, 1], F32, name="inv", bufs=12)
+                nc.vector.reciprocal(out=inv[(s, c)][:, 0:tiles, :], in_=y_bank[c][s % Y_BANKS][:, 0:tiles, E - 1:E])
 
-        def finish(i, c, on_vector):
-            pr, n0, w = QUERY_CHUNKS[i]
+        def finish(s, c, on_vector):
+            i, m0, w = QUERY_PARTS[s]
+            pr, n0 = QUERY_CHUNKS[i][0:2]
             tiles = w // P
-            bank = y_bank[c][i % Y_BANKS]
+            bank = y_bank[c][s % Y_BANKS]
             result = work.tile([P, tiles, E], F32, name="result", bufs=8)
             if on_vector:
                 nc.vector.tensor_tensor(out=result[:], in0=bank[:, 0:tiles, :],
-                                        in1=inv[(i, c)][:, 0:tiles, :].to_broadcast([P, tiles, E]), op=ALU.mult)
+                                        in1=inv[(s, c)][:, 0:tiles, :].to_broadcast([P, tiles, E]), op=ALU.mult)
             else:
                 for a in range(tiles):
-                    nc.scalar.activation(out=result[:, a, :], in_=bank[:, a, :], func=ACT.Copy, scale=inv[(i, c)][:, a, :])
-            nc.sync.dma_start(out=out[2 * pr + c, n0:n0 + w, :].rearrange("(a r) e -> r a e", r=P), in_=result[:])
+                    nc.scalar.activation(out=result[:, a, :], in_=bank[:, a, :], func=ACT.Copy, scale=inv[(s, c)][:, a, :])
+            nc.sync.dma_start(out=out[2 * pr + c, n0 + m0:n0 + m0 + w, :].rearrange("(a r) e -> r a e", r=P), in_=result[:])
 
         def query_weight_abs():
-            nc.vector.tensor_scalar(out=qa_step[:, 0:PACK], in0=qa_sb[:, 0:PACK], scalar1=0.0, scalar2=2.0 / N, op0=ALU.is_ge, op1=ALU.mult)
+            nc.vector.tensor_scalar(out=qa_step[:, 0:HALVES], in0=qa_row[:, 0:HALVES], scalar1=0.0, scalar2=2.0 / N, op0=ALU.is_ge, op1=ALU.mult)
             nc.vector.scalar_tensor_tensor(out=qa_abs[:, 0:PACK], in0=qa_sb[:, 0:PACK], scalar=-1.0, in1=qa_sb[:, 0:PACK], op0=ALU.mult, op1=ALU.max)
 
         def query_weight_sign():
-            nc.vector.tensor_scalar(out=qa_sign[:, 0:PACK], in0=qa_step[:, 0:PACK], scalar1=-1.0 / N, scalar2=None, op0=ALU.add)
+            nc.vector.tensor_scalar(out=qa_sign[:, 0:HALVES], in0=qa_step[:, 0:HALVES], scalar1=-1.0 / N, scalar2=None, op0=ALU.add)
 
-        key_relu(0, True, 0, D // 2)
-        key_exp(0, 0, D // 2)
-        key_exp(0, D // 2, D)
-        key_relu(0, False, D // 2, D)
-        key_weight(0)
-        key_phi(0, 0, D // 2)
-        key_weight(1)
+        key_exp(0)
+        key_relu(0, True)
+        key_weight(1, False)
         key_exp(1)
-        key_exp(2)
-        key_round(0, 0, D // 2)
-        key_relu(3, False)
-        key_phi(0, D // 2, D)
+        key_weight(0, True)
+        key_phi(0)
         key_relu(1, True)
-        key_exp(3)
-        value_round(1, False)
+        key_round(0)
         key_relu(2, True)
+        key_exp(2)
         key_phi(1)
         key_phi(2)
-        value_round(3, False)
-        value_round(2, False)
-        key_exp(4)
         key_round(1)
-        key_relu(4, False)
-        key_exp(5)
-        key_phi(3)
-        key_round(0, D // 2, D)
-        key_relu(6, False)
-        query_weight_abs()
-        key_relu(5, False)
+        key_exp(3)
+        key_relu(3, False)
+        key_relu(4, True)
         key_round(2)
-        key_exp(6)
-        key_round(3)
-        key_phi(4)
-        key_quant(0, 0)
-        query_weight_sign()
-        key_quant(0, 1)
-        key_phi(5)
-        key_round(4)
-        key_phi(6)
+        key_exp(4)
+        key_phi(3)
         value_round(0, False)
-        key_relu(7, False)
+        key_quant(0)
+        key_phi(4)
+        value_quant(0)
+        key_round(4)
+        value_round(1, True)
+        key_relu(5, False)
+        key_round(3)
+        key_exp(5)
+        query_weight_abs()
+        value_quant(1)
+        key_phi(5)
+        key_exp(6)
+        key_quant(1)
         key_round(5)
+        key_relu(6, False)
+        query_weight_sign()
+        key_phi(6)
         query_exp(0)
-        key_round(6)
-        value_quant(0, 0)
-        value_quant(0, 1)
-        key_exp(7)
-        query_relu(0, False)
-        query_clip(0)
-        query_exp(1)
-        query_exp(3)
-        key_phi(7)
-        query_round(0)
-        query_relu(1, False)
-        query_exp(4)
-        state_matmul(0)
-        key_round(7)
-        key_quant(1, 0)
-        state_round(0)
-        value_round(5, False)
-        value_round(7, False)
-        query_clip(1)
-        query_quant(0)
-        value_round(4, False)
-        value_round(6, False)
-        query_exp(2)
-        state_quant(0)
-        query_round(1)
-        query_relu(2, False)
-        query_matmul(0)
-        query_relu(5, False)
-        query_clip(3)
-        invert(0)
-        key_quant(1, 1)
-        finish(0, 1, False)
-        value_quant(1, 1)
-        query_clip(2)
-        query_quant(1)
-        value_quant(1, 0)
         state_matmul(1)
-        query_round(2)
-        state_round(1)
+        value_round(3, True)
+        key_round(6)
+        state_matmul(0)
+        value_round(2, False)
+        state_evict(0, False)
+        value_quant(3)
+        query_exp(1)
+        key_quant(2)
+        query_exp(3)
+        state_park(0)
+        query_relu(1, False)
+        state_fetch(0)
+        value_quant(2)
+        key_quant(3)
+        state_matmul(2)
+        query_clip(1)
+        state_matmul(3)
+        state_evict(1, False)
+        query_relu(0, False)
+        state_park(1)
+        query_exp(2)
+        state_round(0, False)
+        query_relu(2, False)
+        state_fetch(1)
+        query_clip(0)
+        query_clip(3)
+        query_round(1)
+        query_round(0)
+        state_quant(0)
+        query_quant(1)
+        query_clip(2)
+        query_exp(4)
         query_matmul(1)
-        query_exp(5)
+        query_quant(0)
         invert(1)
-        query_quant(2)
         query_relu(3, False)
+        state_round(1, True)
+        query_round(2)
+        query_matmul(0)
+        invert(0)
         state_quant(1)
-        query_matmul(2)
-        finish(0, 0, False)
+        query_quant(2)
         finish(1, 1, False)
-        query_round(3)
-        invert(2)
-        query_clip(4)
         finish(1, 0, False)
-        query_clip(5)
-        query_quant(3)
-        query_matmul(3)
-        query_round(5)
-        invert(3)
+        query_round(3)
+        finish(0, 0, False)
+        query_clip(4)
+        query_matmul(2)
+        finish(0, 1, False)
         query_relu(4, False)
+        invert(2)
         finish(2, 1, False)
-        query_round(4)
+        query_quant(3)
+        query_round(5)
         finish(2, 0, False)
+        query_matmul(3)
+        query_round(4)
+        invert(3)
         query_quant(5)
-        finish(3, 1, False)
+        finish(3, 0, True)
         query_matmul(5)
         query_quant(4)
+        finish(3, 1, True)
         query_matmul(4)
         invert(5)
-        invert(4)
-        finish(3, 0, False)
         finish(5, 1, False)
+        invert(4)
         finish(5, 0, False)
-        finish(4, 1, True)
-        finish(4, 0, False)
+        finish(4, 1, False)
+        finish(4, 0, True)

@@ -15,14 +15,20 @@ ACT = mybir.ActivationFunctionType
 
 P = 128
 PACK = 4
-RUN = 4
 ROWS = D // PACK
 PASSES = N // (P * PACK)
 HALVES = D // P
+RUN = 4
 Y_BANKS = 3
-KEY_PIECES = [(0, 0, 1, 0, 128), (0, 0, 1, 128, 256), (0, 1, 2, 0, 256), (1, 0, 1, 0, 256), (1, 1, 2, 0, 256), (2, 0, 2, 0, 256), (3, 0, 2, 0, 256)]
+MAP_BUFS = 4
+RESULT_BUFS = 8
+
+KEY_PIECES = [(0, 0, 1, 0, 128), (0, 0, 1, 128, 256), (0, 1, 2, 0, 256), (1, 0, 1, 0, 256), (1, 1, 2, 0, 256),
+              (2, 0, 2, 0, 256), (3, 0, 2, 0, 256)]
 QUERY_CHUNKS = [(0, 0, 512), (0, 512, 512), (1, 0, 512), (1, 512, 256), (1, 768, 256)]
 QUERY_PARTS = [(0, 0, 512), (1, 0, 512), (2, 0, 512), (3, 0, 256), (4, 0, 128), (4, 128, 128)]
+
+SCALAR, VECTOR = "scalar", "vector"
 
 
 def tile_rows_lin_elu1_norm_kernel(tc, q, qa, ka, k, t, v, out):
@@ -33,33 +39,45 @@ def tile_rows_lin_elu1_norm_kernel(tc, q, qa, ka, k, t, v, out):
         psum = ctx.enter_context(tc.psum_pool(name="psum", bufs=1))
         ctx.enter_context(tc.manual_schedule())
 
-        zero = keep.tile([P, 8], F32, name="zero")
-        one = keep.tile([P, 8], F32, name="one")
+        zero = keep.tile([P, 1], F32, name="zero")
+        one = keep.tile([P, 1], F32, name="one")
         t_sb = keep.tile([P, PASSES, PACK], F32, name="t_sb")
         ka_sb = keep.tile([P, D], F32, name="ka_sb")
-        qa_sb = keep.tile([P, 8], F32, name="qa_sb")
-        qa_abs = keep.tile([P, 8], F32, name="qa_abs")
-        qa_row = keep.tile([P, 8], F32, name="qa_row")
-        qa_step = keep.tile([P, 8], F32, name="qa_step")
-        qa_sign = keep.tile([P, 8], F32, name="qa_sign")
+        qa_word = keep.tile([P, PACK], F32, name="qa_word")
+        qa_abs = keep.tile([P, PACK], F32, name="qa_abs")
+        qa_row = keep.tile([P, HALVES], F32, name="qa_row")
+        qa_step = keep.tile([P, HALVES], F32, name="qa_step")
+        state_scale = keep.tile([P, HALVES], F32, name="state_scale")
         weight = [keep.tile([P, PACK, D], F32, name="weight%d" % g) for g in range(PASSES)]
-        k_raw = [keep.tile([P, g1 - g0, PACK, hi - lo], F32, name="k_raw%d" % u) for u, (h, g0, g1, lo, hi) in enumerate(KEY_PIECES)]
+        k_raw = [keep.tile([P, g1 - g0, PACK, d1 - d0], F32, name="k_raw%d" % u) for u, (h, g0, g1, d0, d1) in enumerate(KEY_PIECES)]
         v_raw = [keep.tile([P, PASSES, PACK, E], F32, name="v_raw%d" % h) for h in range(H)]
-        q_raw = [keep.tile([P, PACK, w], F32, name="q_raw%d" % i) for i, (pr, n0, w) in enumerate(QUERY_CHUNKS)]
+        q_raw = [keep.tile([P, PACK, w], F32, name="q_raw%d" % i) for i, (pair, n0, w) in enumerate(QUERY_CHUNKS)]
         k_codes = [keep.tile([P, PASSES * D], U32, name="k_codes%d" % h, align_bytes=64) for h in range(H)]
         k_scales = [keep.tile([P, PASSES * D], U8, name="k_scales%d" % h, align_bytes=64) for h in range(H)]
         v_codes = [keep.tile([P, PASSES * E], U32, name="v_codes%d" % h, align_bytes=64) for h in range(H)]
         v_scales = [keep.tile([P, PASSES * E], U8, name="v_scales%d" % h, align_bytes=64) for h in range(H)]
-        s_codes = [keep.tile([P, E], U32, name="s_codes%d" % pr, align_bytes=64) for pr in range(2)]
-        s_scales = [keep.tile([P, E], U8, name="s_scales%d" % pr, align_bytes=64) for pr in range(2)]
-        s_bank = [psum.tile([P, 2 * HALVES, E], F32, name="s_bank%d" % pr) for pr in range(2)]
+        s_codes = [keep.tile([P, E], U32, name="s_codes%d" % pair, align_bytes=64) for pair in range(2)]
+        s_scales = [keep.tile([P, E], U8, name="s_scales%d" % pair, align_bytes=64) for pair in range(2)]
+        s_bank = [psum.tile([P, 2 * HALVES, E], F32, name="s_bank%d" % pair) for pair in range(2)]
         y_bank = [[psum.tile([P, 4, E], F32, name="y_bank%d_%d" % (c, b)) for b in range(Y_BANKS)] for c in range(2)]
 
+        def interleaved(words):
+            return words.rearrange("p (b i) j -> p b j i", i=RUN)
+
+        def by_code(rows):
+            return rows.rearrange("p j (b i) -> p b j i", i=RUN)
+
+        def round_copy(dst, src, engine):
+            if engine == VECTOR:
+                nc.vector.tensor_copy(out=interleaved(dst), in_=by_code(src))
+            else:
+                nc.scalar.activation(out=interleaved(dst), in_=by_code(src), func=ACT.Copy)
+
         def load_k(u):
-            h, g0, g1, lo, hi = KEY_PIECES[u]
+            h, g0, g1, d0, d1 = KEY_PIECES[u]
             src = k[h].rearrange("(g p j) d -> p g j d", g=PASSES, j=PACK)
             if g1 - g0 == 1:
-                nc.sync.dma_start(out=k_raw[u][:, 0], in_=src[:, g0, :, lo:hi])
+                nc.sync.dma_start(out=k_raw[u][:, 0], in_=src[:, g0, :, d0:d1])
             else:
                 nc.sync.dma_start(out=k_raw[u][:].rearrange("p g j d -> p g (j d)"), in_=src.rearrange("p g j d -> p g (j d)"))
 
@@ -68,32 +86,27 @@ def tile_rows_lin_elu1_norm_kernel(tc, q, qa, ka, k, t, v, out):
                               in_=v[h].rearrange("(g p j) e -> p g (j e)", g=PASSES, j=PACK))
 
         def load_q(i):
-            pr, n0, w = QUERY_CHUNKS[i]
-            src = q[2 * pr:2 * pr + 2].rearrange("c (p j) n -> (c p) j n", j=PACK)
+            pair, n0, w = QUERY_CHUNKS[i]
+            src = q[2 * pair:2 * pair + 2].rearrange("c (p j) n -> (c p) j n", j=PACK)
             nc.sync.dma_start(out=q_raw[i][:], in_=src[:, :, n0:n0 + w])
 
         load_k(0)
         nc.sync.dma_start(out=ka_sb[:], in_=ka)
         nc.sync.dma_start(out=t_sb[:], in_=t.rearrange("(g p j) o -> p g (j o)", g=PASSES, j=PACK))
-        load_k(1)
-        load_k(2)
-        load_k(3)
-        load_k(4)
+        for u in range(1, 5):
+            load_k(u)
         load_v(0)
         load_k(5)
         load_v(1)
         for c in range(2):
-            nc.sync.dma_start(out=qa_sb[c * ROWS:(c + 1) * ROWS, 0:PACK], in_=qa.rearrange("(p j) o -> p (j o)", j=PACK))
-        with nc.allow_non_contiguous_dma(reason="one weight a partition"):
-            nc.sync.dma_start(out=qa_row[:, 0:HALVES], in_=qa.rearrange("(u r) o -> r (u o)", r=P))
+            nc.sync.dma_start(out=qa_word[c * ROWS:(c + 1) * ROWS, :], in_=qa.rearrange("(p j) o -> p (j o)", j=PACK))
+        with nc.allow_non_contiguous_dma(reason="one weight for each row of the state"):
+            nc.sync.dma_start(out=qa_row[:], in_=qa.rearrange("(u r) o -> r (u o)", r=P))
         load_k(6)
         load_v(2)
         load_v(3)
-        load_q(0)
-        load_q(1)
-        load_q(2)
-        load_q(3)
-        load_q(4)
+        for i in range(len(QUERY_CHUNKS)):
+            load_q(i)
 
         nc.gpsimd.memset(zero[:], 0.0)
         nc.scalar.activation(out=one[:], in_=zero[:], func=ACT.Exp)
@@ -101,50 +114,46 @@ def tile_rows_lin_elu1_norm_kernel(tc, q, qa, ka, k, t, v, out):
         k_exp, k_pos, k_bf, v_bf = {}, {}, {}, {}
 
         def key_exp(u):
-            k_exp[u] = work.tile(k_raw[u].shape, F32, name="k_exp", tag="expo", bufs=4)
+            k_exp[u] = work.tile(k_raw[u].shape, F32, name="k_exp", tag="expo", bufs=MAP_BUFS)
             nc.scalar.activation(out=k_exp[u][:], in_=k_raw[u][:], func=ACT.Exp)
 
-        def key_relu(u, on_vector):
-            k_pos[u] = work.tile(k_raw[u].shape, F32, name="k_pos", tag="pos", bufs=4)
-            if on_vector:
+        def key_relu(u, engine):
+            k_pos[u] = work.tile(k_raw[u].shape, F32, name="k_pos", tag="pos", bufs=MAP_BUFS)
+            if engine == VECTOR:
                 nc.vector.tensor_scalar(out=k_pos[u][:], in0=k_raw[u][:], scalar1=0.0, scalar2=None, op0=ALU.max)
             else:
                 nc.scalar.activation(out=k_pos[u][:], in_=k_raw[u][:], func=ACT.Relu)
 
-        def key_weight(g, on_vector):
+        def key_weight(g, engine):
             for j in range(PACK):
-                if on_vector:
+                if engine == VECTOR:
                     nc.vector.tensor_scalar(out=weight[g][:, j, :], in0=ka_sb[:], scalar1=t_sb[:, g, j:j + 1], scalar2=None, op0=ALU.mult)
                 else:
                     nc.scalar.activation(out=weight[g][:, j, :], in_=ka_sb[:], func=ACT.Copy, scale=t_sb[:, g, j:j + 1])
 
         def key_phi(u):
-            nc.vector.scalar_tensor_tensor(out=k_exp[u][:], in0=k_exp[u][:], scalar=one[:, 0:1], in1=k_pos[u][:], op0=ALU.min, op1=ALU.add)
+            nc.vector.scalar_tensor_tensor(out=k_exp[u][:], in0=k_exp[u][:], scalar=one[:], in1=k_pos[u][:], op0=ALU.min, op1=ALU.add)
 
         def key_round(u):
-            h, g0, g1, lo, hi = KEY_PIECES[u]
+            h, g0, g1, d0, d1 = KEY_PIECES[u]
             if h not in k_bf:
                 k_bf[h] = work.tile([P, PASSES, D, PACK], BF16, name="k_bf", align_bytes=64)
             for g in range(g0, g1):
-                nc.vector.tensor_tensor(out=k_bf[h][:, g, lo:hi, :].rearrange("p (b i) j -> p b j i", i=RUN),
-                                        in0=k_exp[u][:, g - g0].rearrange("p j (b i) -> p b j i", i=RUN),
-                                        in1=weight[g][:, :, lo:hi].rearrange("p j (b i) -> p b j i", i=RUN), op=ALU.mult)
+                nc.vector.tensor_tensor(out=interleaved(k_bf[h][:, g, d0:d1, :]), in0=by_code(k_exp[u][:, g - g0]),
+                                        in1=by_code(weight[g][:, :, d0:d1]), op=ALU.mult)
 
         def key_quant(h):
             nc.vector.quantize_mx(out=k_codes[h][:].bitcast(FP8X4), scales=k_scales[h][:], in_=k_bf[h][:].rearrange("p g d j -> p (g d j)"))
 
-        def value_round(h, on_vector):
+        def value_round(h, engine):
             v_bf[h] = work.tile([P, PASSES, E, PACK], BF16, name="v_bf", align_bytes=64)
             for g in range(PASSES):
-                dst = v_bf[h][:, g].rearrange("p (b i) j -> p b j i", i=RUN)
-                src = v_raw[h][:, g].rearrange("p j (b i) -> p b j i", i=RUN)
-                if on_vector:
-                    nc.vector.tensor_copy(out=dst, in_=src)
-                else:
-                    nc.scalar.activation(out=dst, in_=src, func=ACT.Copy)
+                round_copy(v_bf[h][:, g], v_raw[h][:, g], engine)
 
         def value_quant(h):
             nc.vector.quantize_mx(out=v_codes[h][:].bitcast(FP8X4), scales=v_scales[h][:], in_=v_bf[h][:].rearrange("p g e j -> p (g e j)"))
+
+        s_out, s_in, s_bf = {}, {}, {}
 
         def state_matmul(h):
             for u in range(HALVES):
@@ -155,55 +164,46 @@ def tile_rows_lin_elu1_norm_kernel(tc, q, qa, ka, k, t, v, out):
                                         rhs=v_codes[h][:, g * E:(g + 1) * E].bitcast(FP8X4), rhs_scale=v_scales[h][:, g * E:(g + 1) * E],
                                         start=(g == 0), stop=(g == PASSES - 1))
 
-        s_out, s_in, s_bf = {}, {}, {}
-
-        def parked(pr):
-            return out[H - 1, pr * 2 * D:(pr + 1) * 2 * D, :]
-
-        def state_evict(pr, on_vector):
-            s_out[pr] = work.tile([P, 2 * HALVES, E], F32, name="s_out")
+        def state_evict(pair):
+            s_out[pair] = work.tile([P, 2 * HALVES, E], F32, name="s_out")
             for a in range(2 * HALVES):
-                sign = qa_sign[:, a % HALVES:a % HALVES + 1]
-                if on_vector:
-                    nc.vector.tensor_scalar(out=s_out[pr][:, a, :], in0=s_bank[pr][:, a, :], scalar1=sign, scalar2=None, op0=ALU.mult)
-                else:
-                    nc.scalar.activation(out=s_out[pr][:, a, :], in_=s_bank[pr][:, a, :], func=ACT.Copy, scale=sign)
+                nc.scalar.activation(out=s_out[pair][:, a, :], in_=s_bank[pair][:, a, :], func=ACT.Copy,
+                                     scale=state_scale[:, a % HALVES:a % HALVES + 1])
 
-        def state_park(pr):
-            nc.sync.dma_start(out=parked(pr).rearrange("(a r) e -> r a e", r=P), in_=s_out[pr][:])
+        def parked(pair):
+            return out[H - 1, pair * 2 * D:(pair + 1) * 2 * D, :]
 
-        def state_fetch(pr):
-            s_in[pr] = work.tile([P, PACK, E], F32, name="s_in")
-            nc.sync.dma_start(out=s_in[pr][:], in_=parked(pr).rearrange("(p x) e -> p x e", x=PACK))
+        def state_park(pair):
+            nc.sync.dma_start(out=parked(pair).rearrange("(a r) e -> r a e", r=P), in_=s_out[pair][:])
 
-        def state_round(pr, on_vector):
-            s_bf[pr] = work.tile([P, E, PACK], BF16, name="s_bf", align_bytes=64)
-            dst = s_bf[pr][:].rearrange("p (b i) x -> p b x i", i=RUN)
-            src = s_in[pr][:].rearrange("p x (b i) -> p b x i", i=RUN)
-            if on_vector:
-                nc.vector.tensor_copy(out=dst, in_=src)
-            else:
-                nc.scalar.activation(out=dst, in_=src, func=ACT.Copy)
+        def state_fetch(pair):
+            s_in[pair] = work.tile([P, PACK, E], F32, name="s_in")
+            nc.sync.dma_start(out=s_in[pair][:], in_=parked(pair).rearrange("(p j) e -> p j e", j=PACK))
 
-        def state_quant(pr):
-            nc.vector.quantize_mx(out=s_codes[pr][:].bitcast(FP8X4), scales=s_scales[pr][:], in_=s_bf[pr][:].rearrange("p e x -> p (e x)"))
+        def state_round(pair, engine):
+            s_bf[pair] = work.tile([P, E, PACK], BF16, name="s_bf", align_bytes=64)
+            round_copy(s_bf[pair][:], s_in[pair][:], engine)
+
+        def state_quant(pair):
+            nc.vector.quantize_mx(out=s_codes[pair][:].bitcast(FP8X4), scales=s_scales[pair][:], in_=s_bf[pair][:].rearrange("p e j -> p (e j)"))
 
         q_exp, q_pos, q_bf, q_codes, q_scales, inv = {}, {}, {}, {}, {}, {}
 
+        def query_weight_abs():
+            nc.vector.tensor_scalar(out=qa_step[:], in0=qa_row[:], scalar1=0.0, scalar2=2.0 / N, op0=ALU.is_ge, op1=ALU.mult)
+            nc.vector.scalar_tensor_tensor(out=qa_abs[:], in0=qa_word[:], scalar=-1.0, in1=qa_word[:], op0=ALU.mult, op1=ALU.max)
+
+        def query_weight_sign():
+            nc.vector.tensor_scalar(out=state_scale[:], in0=qa_step[:], scalar1=-1.0 / N, scalar2=None, op0=ALU.add)
+
         def query_exp(i):
-            w = QUERY_CHUNKS[i][2]
-            q_exp[i] = work.tile([P, PACK, w], F32, name="q_exp", tag="expo", bufs=4)
+            q_exp[i] = work.tile([P, PACK, QUERY_CHUNKS[i][2]], F32, name="q_exp", tag="expo", bufs=MAP_BUFS)
             nc.scalar.activation(out=q_exp[i][:], in_=q_raw[i][:], func=ACT.Exp)
 
-        def query_relu(i, on_vector):
-            w = QUERY_CHUNKS[i][2]
-            q_pos[i] = work.tile([P, PACK, w], F32, name="q_pos", tag="pos", bufs=4)
+        def query_relu(i):
+            q_pos[i] = work.tile([P, PACK, QUERY_CHUNKS[i][2]], F32, name="q_pos", tag="pos", bufs=MAP_BUFS)
             for j in range(PACK):
-                if on_vector:
-                    nc.vector.tensor_scalar(out=q_pos[i][:, j, :], in0=q_raw[i][:, j, :], scalar1=0.0, scalar2=qa_abs[:, j:j + 1],
-                                            op0=ALU.max, op1=ALU.mult)
-                else:
-                    nc.scalar.activation(out=q_pos[i][:, j, :], in_=q_raw[i][:, j, :], func=ACT.Relu, scale=qa_abs[:, j:j + 1])
+                nc.scalar.activation(out=q_pos[i][:, j, :], in_=q_raw[i][:, j, :], func=ACT.Relu, scale=qa_abs[:, j:j + 1])
 
         def query_clip(i):
             for j in range(PACK):
@@ -213,9 +213,8 @@ def tile_rows_lin_elu1_norm_kernel(tc, q, qa, ka, k, t, v, out):
         def query_round(s):
             i, m0, w = QUERY_PARTS[s]
             q_bf[s] = work.tile([P, w, PACK], BF16, name="q_bf", align_bytes=64)
-            nc.vector.tensor_tensor(out=q_bf[s][:].rearrange("p (b i) j -> p b j i", i=RUN),
-                                    in0=q_exp[i][:, :, m0:m0 + w].rearrange("p j (b i) -> p b j i", i=RUN),
-                                    in1=q_pos[i][:, :, m0:m0 + w].rearrange("p j (b i) -> p b j i", i=RUN), op=ALU.add)
+            nc.vector.tensor_tensor(out=interleaved(q_bf[s][:]), in0=by_code(q_exp[i][:, :, m0:m0 + w]),
+                                    in1=by_code(q_pos[i][:, :, m0:m0 + w]), op=ALU.add)
 
         def query_quant(s):
             w = QUERY_PARTS[s][2]
@@ -225,68 +224,60 @@ def tile_rows_lin_elu1_norm_kernel(tc, q, qa, ka, k, t, v, out):
 
         def query_matmul(s):
             i, m0, w = QUERY_PARTS[s]
-            pr = QUERY_CHUNKS[i][0]
+            pair = QUERY_CHUNKS[i][0]
             for a in range(w // P):
                 for c in range(2):
                     rows = slice(c * ROWS, (c + 1) * ROWS)
                     nc.tensor.matmul_mx(out=y_bank[c][s % Y_BANKS][:, a, :], lhsT=q_codes[s][rows, a * P:(a + 1) * P].bitcast(FP8X4),
                                         lhsT_scale=q_scales[s][rows, a * P:(a + 1) * P],
-                                        rhs=s_codes[pr][rows, :].bitcast(FP8X4), rhs_scale=s_scales[pr][rows, :],
+                                        rhs=s_codes[pair][rows, :].bitcast(FP8X4), rhs_scale=s_scales[pair][rows, :],
                                         start=True, stop=True)
 
         def invert(s):
             tiles = QUERY_PARTS[s][2] // P
             for c in range(2):
-                inv[(s, c)] = work.tile([P, 8, 1], F32, name="inv", bufs=12)
-                nc.vector.reciprocal(out=inv[(s, c)][:, 0:tiles, :], in_=y_bank[c][s % Y_BANKS][:, 0:tiles, E - 1:E])
+                inv[(s, c)] = work.tile([P, tiles, 1], F32, name="inv", bufs=2 * len(QUERY_PARTS))
+                nc.vector.reciprocal(out=inv[(s, c)][:], in_=y_bank[c][s % Y_BANKS][:, 0:tiles, E - 1:E])
 
-        def finish(s, c, on_vector):
+        def finish(s, c, engine):
             i, m0, w = QUERY_PARTS[s]
-            pr, n0 = QUERY_CHUNKS[i][0:2]
+            pair, n0 = QUERY_CHUNKS[i][0:2]
             tiles = w // P
             bank = y_bank[c][s % Y_BANKS]
-            result = work.tile([P, tiles, E], F32, name="result", bufs=8)
-            if on_vector:
-                nc.vector.tensor_tensor(out=result[:], in0=bank[:, 0:tiles, :],
-                                        in1=inv[(s, c)][:, 0:tiles, :].to_broadcast([P, tiles, E]), op=ALU.mult)
+            result = work.tile([P, tiles, E], F32, name="result", bufs=RESULT_BUFS)
+            if engine == VECTOR:
+                nc.vector.tensor_tensor(out=result[:], in0=bank[:, 0:tiles, :], in1=inv[(s, c)][:].to_broadcast([P, tiles, E]), op=ALU.mult)
             else:
                 for a in range(tiles):
                     nc.scalar.activation(out=result[:, a, :], in_=bank[:, a, :], func=ACT.Copy, scale=inv[(s, c)][:, a, :])
-            nc.sync.dma_start(out=out[2 * pr + c, n0 + m0:n0 + m0 + w, :].rearrange("(a r) e -> r a e", r=P), in_=result[:])
-
-        def query_weight_abs():
-            nc.vector.tensor_scalar(out=qa_step[:, 0:HALVES], in0=qa_row[:, 0:HALVES], scalar1=0.0, scalar2=2.0 / N, op0=ALU.is_ge, op1=ALU.mult)
-            nc.vector.scalar_tensor_tensor(out=qa_abs[:, 0:PACK], in0=qa_sb[:, 0:PACK], scalar=-1.0, in1=qa_sb[:, 0:PACK], op0=ALU.mult, op1=ALU.max)
-
-        def query_weight_sign():
-            nc.vector.tensor_scalar(out=qa_sign[:, 0:HALVES], in0=qa_step[:, 0:HALVES], scalar1=-1.0 / N, scalar2=None, op0=ALU.add)
+            nc.sync.dma_start(out=out[2 * pair + c, n0 + m0:n0 + m0 + w, :].rearrange("(a r) e -> r a e", r=P), in_=result[:])
 
         key_exp(0)
-        key_relu(0, True)
-        key_weight(1, False)
+        key_relu(0, VECTOR)
+        key_weight(1, SCALAR)
         key_exp(1)
-        key_weight(0, True)
+        key_weight(0, VECTOR)
         key_phi(0)
-        key_relu(1, True)
+        key_relu(1, VECTOR)
         key_round(0)
-        key_relu(2, True)
+        key_relu(2, VECTOR)
         key_exp(2)
         key_phi(1)
         key_phi(2)
         key_round(1)
         key_exp(3)
-        key_relu(3, False)
-        key_relu(4, True)
+        key_relu(3, SCALAR)
+        key_relu(4, VECTOR)
         key_round(2)
         key_exp(4)
         key_phi(3)
-        value_round(0, False)
+        value_round(0, SCALAR)
         key_quant(0)
         key_phi(4)
         value_quant(0)
         key_round(4)
-        value_round(1, True)
-        key_relu(5, False)
+        value_round(1, VECTOR)
+        key_relu(5, SCALAR)
         key_round(3)
         key_exp(5)
         query_weight_abs()
@@ -295,34 +286,34 @@ def tile_rows_lin_elu1_norm_kernel(tc, q, qa, ka, k, t, v, out):
         key_exp(6)
         key_quant(1)
         key_round(5)
-        key_relu(6, False)
+        key_relu(6, SCALAR)
         query_weight_sign()
         key_phi(6)
         query_exp(0)
         state_matmul(1)
-        value_round(3, True)
+        value_round(3, VECTOR)
         key_round(6)
         state_matmul(0)
-        value_round(2, False)
-        state_evict(0, False)
+        value_round(2, SCALAR)
+        state_evict(0)
         value_quant(3)
         query_exp(1)
         key_quant(2)
         query_exp(3)
         state_park(0)
-        query_relu(1, False)
+        query_relu(1)
         state_fetch(0)
         value_quant(2)
         key_quant(3)
         state_matmul(2)
         query_clip(1)
         state_matmul(3)
-        state_evict(1, False)
-        query_relu(0, False)
+        state_evict(1)
+        query_relu(0)
         state_park(1)
         query_exp(2)
-        state_round(0, False)
-        query_relu(2, False)
+        state_round(0, SCALAR)
+        query_relu(2)
         state_fetch(1)
         query_clip(0)
         query_clip(3)
@@ -335,38 +326,38 @@ def tile_rows_lin_elu1_norm_kernel(tc, q, qa, ka, k, t, v, out):
         query_matmul(1)
         query_quant(0)
         invert(1)
-        query_relu(3, False)
-        state_round(1, True)
+        query_relu(3)
+        state_round(1, VECTOR)
         query_round(2)
         query_matmul(0)
         invert(0)
         state_quant(1)
         query_quant(2)
-        finish(1, 1, False)
-        finish(1, 0, False)
+        finish(1, 1, SCALAR)
+        finish(1, 0, SCALAR)
         query_round(3)
-        finish(0, 0, False)
+        finish(0, 0, SCALAR)
         query_clip(4)
         query_matmul(2)
-        finish(0, 1, False)
-        query_relu(4, False)
+        finish(0, 1, SCALAR)
+        query_relu(4)
         invert(2)
-        finish(2, 1, False)
+        finish(2, 1, SCALAR)
         query_quant(3)
         query_round(5)
-        finish(2, 0, False)
+        finish(2, 0, SCALAR)
         query_matmul(3)
         query_round(4)
-        invert(3)
         query_quant(5)
-        finish(3, 0, True)
+        invert(3)
+        finish(3, 0, SCALAR)
         query_matmul(5)
         query_quant(4)
-        finish(3, 1, True)
+        finish(3, 1, SCALAR)
         query_matmul(4)
         invert(5)
-        finish(5, 1, False)
+        finish(5, 1, SCALAR)
         invert(4)
-        finish(5, 0, False)
-        finish(4, 1, False)
-        finish(4, 0, True)
+        finish(5, 0, SCALAR)
+        finish(4, 1, SCALAR)
+        finish(4, 0, VECTOR)

from contextlib import ExitStack

import concourse.mybir as mybir

H, D, N, E = 4, 256, 1024, 128
FLOPS = 2 * 2 * H * N * D * E

F32 = mybir.dt.float32
BF16 = mybir.dt.bfloat16
U32 = mybir.dt.uint32
U8 = mybir.dt.uint8
FP8X4 = mybir.dt.float8_e4m3fn_x4
ALU = mybir.AluOpType
ACT = mybir.ActivationFunctionType

P = 128
PACK = 4
ROWS = D // PACK
PASSES = N // (P * PACK)
HALVES = D // P
RUN = 4
Y_BANKS = 3
MAP_BUFS = 4
RESULT_BUFS = 8

KEY_PIECES = [(0, 0, 1, 0, 128), (0, 0, 1, 128, 256), (0, 1, 2, 0, 256), (1, 0, 1, 0, 256), (1, 1, 2, 0, 256),
              (2, 0, 2, 0, 256), (3, 0, 2, 0, 256)]
QUERY_CHUNKS = [(0, 0, 512), (0, 512, 512), (1, 0, 512), (1, 512, 256), (1, 768, 256)]
QUERY_PARTS = [(0, 0, 512), (1, 0, 512), (2, 0, 512), (3, 0, 256), (4, 0, 128), (4, 128, 128)]

SCALAR, VECTOR = "scalar", "vector"


def tile_rows_lin_elu1_norm_kernel(tc, q, qa, ka, k, t, v, out):
    nc = tc.nc
    with ExitStack() as ctx:
        keep = ctx.enter_context(tc.tile_pool(name="keep", bufs=1))
        work = ctx.enter_context(tc.tile_pool(name="work", bufs=2))
        psum = ctx.enter_context(tc.psum_pool(name="psum", bufs=1))
        ctx.enter_context(tc.manual_schedule())

        zero = keep.tile([P, 1], F32, name="zero")
        one = keep.tile([P, 1], F32, name="one")
        t_sb = keep.tile([P, PASSES, PACK], F32, name="t_sb")
        ka_sb = keep.tile([P, D], F32, name="ka_sb")
        qa_word = keep.tile([P, PACK], F32, name="qa_word")
        qa_abs = keep.tile([P, PACK], F32, name="qa_abs")
        qa_row = keep.tile([P, HALVES], F32, name="qa_row")
        qa_step = keep.tile([P, HALVES], F32, name="qa_step")
        state_scale = keep.tile([P, HALVES], F32, name="state_scale")
        weight = [keep.tile([P, PACK, D], F32, name="weight%d" % g) for g in range(PASSES)]
        k_raw = [keep.tile([P, g1 - g0, PACK, d1 - d0], F32, name="k_raw%d" % u) for u, (h, g0, g1, d0, d1) in enumerate(KEY_PIECES)]
        v_raw = [keep.tile([P, PASSES, PACK, E], F32, name="v_raw%d" % h) for h in range(H)]
        q_raw = [keep.tile([P, PACK, w], F32, name="q_raw%d" % i) for i, (pair, n0, w) in enumerate(QUERY_CHUNKS)]
        k_codes = [keep.tile([P, PASSES * D], U32, name="k_codes%d" % h, align_bytes=64) for h in range(H)]
        k_scales = [keep.tile([P, PASSES * D], U8, name="k_scales%d" % h, align_bytes=64) for h in range(H)]
        v_codes = [keep.tile([P, PASSES * E], U32, name="v_codes%d" % h, align_bytes=64) for h in range(H)]
        v_scales = [keep.tile([P, PASSES * E], U8, name="v_scales%d" % h, align_bytes=64) for h in range(H)]
        s_codes = [keep.tile([P, E], U32, name="s_codes%d" % pair, align_bytes=64) for pair in range(2)]
        s_scales = [keep.tile([P, E], U8, name="s_scales%d" % pair, align_bytes=64) for pair in range(2)]
        s_bank = [psum.tile([P, 2 * HALVES, E], F32, name="s_bank%d" % pair) for pair in range(2)]
        y_bank = [[psum.tile([P, 4, E], F32, name="y_bank%d_%d" % (c, b)) for b in range(Y_BANKS)] for c in range(2)]

        def interleaved(words):
            return words.rearrange("p (b i) j -> p b j i", i=RUN)

        def by_code(rows):
            return rows.rearrange("p j (b i) -> p b j i", i=RUN)

        def round_copy(dst, src, engine):
            if engine == VECTOR:
                nc.vector.tensor_copy(out=interleaved(dst), in_=by_code(src))
            else:
                nc.scalar.activation(out=interleaved(dst), in_=by_code(src), func=ACT.Copy)

        def load_k(u):
            h, g0, g1, d0, d1 = KEY_PIECES[u]
            src = k[h].rearrange("(g p j) d -> p g j d", g=PASSES, j=PACK)
            if g1 - g0 == 1:
                nc.sync.dma_start(out=k_raw[u][:, 0], in_=src[:, g0, :, d0:d1])
            else:
                nc.sync.dma_start(out=k_raw[u][:].rearrange("p g j d -> p g (j d)"), in_=src.rearrange("p g j d -> p g (j d)"))

        def load_v(h):
            nc.sync.dma_start(out=v_raw[h][:].rearrange("p g j e -> p g (j e)"),
                              in_=v[h].rearrange("(g p j) e -> p g (j e)", g=PASSES, j=PACK))

        def load_q(i):
            pair, n0, w = QUERY_CHUNKS[i]
            src = q[2 * pair:2 * pair + 2].rearrange("c (p j) n -> (c p) j n", j=PACK)
            nc.sync.dma_start(out=q_raw[i][:], in_=src[:, :, n0:n0 + w])

        load_k(0)
        nc.sync.dma_start(out=ka_sb[:], in_=ka)
        nc.sync.dma_start(out=t_sb[:], in_=t.rearrange("(g p j) o -> p g (j o)", g=PASSES, j=PACK))
        for u in range(1, 5):
            load_k(u)
        load_v(0)
        load_k(5)
        load_v(1)
        for c in range(2):
            nc.sync.dma_start(out=qa_word[c * ROWS:(c + 1) * ROWS, :], in_=qa.rearrange("(p j) o -> p (j o)", j=PACK))
        with nc.allow_non_contiguous_dma(reason="one weight for each row of the state"):
            nc.sync.dma_start(out=qa_row[:], in_=qa.rearrange("(u r) o -> r (u o)", r=P))
        load_k(6)
        load_v(2)
        load_v(3)
        for i in range(len(QUERY_CHUNKS)):
            load_q(i)

        nc.gpsimd.memset(zero[:], 0.0)
        nc.scalar.activation(out=one[:], in_=zero[:], func=ACT.Exp)

        k_exp, k_pos, k_bf, v_bf = {}, {}, {}, {}

        def key_exp(u):
            k_exp[u] = work.tile(k_raw[u].shape, F32, name="k_exp", tag="expo", bufs=MAP_BUFS)
            nc.scalar.activation(out=k_exp[u][:], in_=k_raw[u][:], func=ACT.Exp)

        def key_relu(u, engine):
            k_pos[u] = work.tile(k_raw[u].shape, F32, name="k_pos", tag="pos", bufs=MAP_BUFS)
            if engine == VECTOR:
                nc.vector.tensor_scalar(out=k_pos[u][:], in0=k_raw[u][:], scalar1=0.0, scalar2=None, op0=ALU.max)
            else:
                nc.scalar.activation(out=k_pos[u][:], in_=k_raw[u][:], func=ACT.Relu)

        def key_weight(g, engine):
            for j in range(PACK):
                if engine == VECTOR:
                    nc.vector.tensor_scalar(out=weight[g][:, j, :], in0=ka_sb[:], scalar1=t_sb[:, g, j:j + 1], scalar2=None, op0=ALU.mult)
                else:
                    nc.scalar.activation(out=weight[g][:, j, :], in_=ka_sb[:], func=ACT.Copy, scale=t_sb[:, g, j:j + 1])

        def key_phi(u):
            nc.vector.scalar_tensor_tensor(out=k_exp[u][:], in0=k_exp[u][:], scalar=one[:], in1=k_pos[u][:], op0=ALU.min, op1=ALU.add)

        def key_round(u):
            h, g0, g1, d0, d1 = KEY_PIECES[u]
            if h not in k_bf:
                k_bf[h] = work.tile([P, PASSES, D, PACK], BF16, name="k_bf", align_bytes=64)
            for g in range(g0, g1):
                nc.vector.tensor_tensor(out=interleaved(k_bf[h][:, g, d0:d1, :]), in0=by_code(k_exp[u][:, g - g0]),
                                        in1=by_code(weight[g][:, :, d0:d1]), op=ALU.mult)

        def key_quant(h):
            nc.vector.quantize_mx(out=k_codes[h][:].bitcast(FP8X4), scales=k_scales[h][:], in_=k_bf[h][:].rearrange("p g d j -> p (g d j)"))

        def value_round(h, engine):
            v_bf[h] = work.tile([P, PASSES, E, PACK], BF16, name="v_bf", align_bytes=64)
            for g in range(PASSES):
                round_copy(v_bf[h][:, g], v_raw[h][:, g], engine)

        def value_quant(h):
            nc.vector.quantize_mx(out=v_codes[h][:].bitcast(FP8X4), scales=v_scales[h][:], in_=v_bf[h][:].rearrange("p g e j -> p (g e j)"))

        s_out, s_in, s_bf = {}, {}, {}

        def state_matmul(h):
            for u in range(HALVES):
                for g in range(PASSES):
                    cols = slice(g * D + u * P, g * D + (u + 1) * P)
                    nc.tensor.matmul_mx(out=s_bank[h // 2][:, (h % 2) * HALVES + u, :], lhsT=k_codes[h][:, cols].bitcast(FP8X4),
                                        lhsT_scale=k_scales[h][:, cols],
                                        rhs=v_codes[h][:, g * E:(g + 1) * E].bitcast(FP8X4), rhs_scale=v_scales[h][:, g * E:(g + 1) * E],
                                        start=(g == 0), stop=(g == PASSES - 1))

        def state_evict(pair):
            s_out[pair] = work.tile([P, 2 * HALVES, E], F32, name="s_out")
            for a in range(2 * HALVES):
                nc.scalar.activation(out=s_out[pair][:, a, :], in_=s_bank[pair][:, a, :], func=ACT.Copy,
                                     scale=state_scale[:, a % HALVES:a % HALVES + 1])

        def parked(pair):
            return out[H - 1, pair * 2 * D:(pair + 1) * 2 * D, :]

        def state_park(pair):
            nc.sync.dma_start(out=parked(pair).rearrange("(a r) e -> r a e", r=P), in_=s_out[pair][:])

        def state_fetch(pair):
            s_in[pair] = work.tile([P, PACK, E], F32, name="s_in")
            nc.sync.dma_start(out=s_in[pair][:], in_=parked(pair).rearrange("(p j) e -> p j e", j=PACK))

        def state_round(pair, engine):
            s_bf[pair] = work.tile([P, E, PACK], BF16, name="s_bf", align_bytes=64)
            round_copy(s_bf[pair][:], s_in[pair][:], engine)

        def state_quant(pair):
            nc.vector.quantize_mx(out=s_codes[pair][:].bitcast(FP8X4), scales=s_scales[pair][:], in_=s_bf[pair][:].rearrange("p e j -> p (e j)"))

        q_exp, q_pos, q_bf, q_codes, q_scales, inv = {}, {}, {}, {}, {}, {}

        def query_weight_abs():
            nc.vector.tensor_scalar(out=qa_step[:], in0=qa_row[:], scalar1=0.0, scalar2=2.0 / N, op0=ALU.is_ge, op1=ALU.mult)
            nc.vector.scalar_tensor_tensor(out=qa_abs[:], in0=qa_word[:], scalar=-1.0, in1=qa_word[:], op0=ALU.mult, op1=ALU.max)

        def query_weight_sign():
            nc.vector.tensor_scalar(out=state_scale[:], in0=qa_step[:], scalar1=-1.0 / N, scalar2=None, op0=ALU.add)

        def query_exp(i):
            q_exp[i] = work.tile([P, PACK, QUERY_CHUNKS[i][2]], F32, name="q_exp", tag="expo", bufs=MAP_BUFS)
            nc.scalar.activation(out=q_exp[i][:], in_=q_raw[i][:], func=ACT.Exp)

        def query_relu(i):
            q_pos[i] = work.tile([P, PACK, QUERY_CHUNKS[i][2]], F32, name="q_pos", tag="pos", bufs=MAP_BUFS)
            for j in range(PACK):
                nc.scalar.activation(out=q_pos[i][:, j, :], in_=q_raw[i][:, j, :], func=ACT.Relu, scale=qa_abs[:, j:j + 1])

        def query_clip(i):
            for j in range(PACK):
                nc.vector.tensor_scalar(out=q_exp[i][:, j, :], in0=q_exp[i][:, j, :], scalar1=1.0, scalar2=qa_abs[:, j:j + 1],
                                        op0=ALU.min, op1=ALU.mult)

        def query_round(s):
            i, m0, w = QUERY_PARTS[s]
            q_bf[s] = work.tile([P, w, PACK], BF16, name="q_bf", align_bytes=64)
            nc.vector.tensor_tensor(out=interleaved(q_bf[s][:]), in0=by_code(q_exp[i][:, :, m0:m0 + w]),
                                    in1=by_code(q_pos[i][:, :, m0:m0 + w]), op=ALU.add)

        def query_quant(s):
            w = QUERY_PARTS[s][2]
            q_codes[s] = work.tile([P, w], U32, name="q_codes", align_bytes=64)
            q_scales[s] = work.tile([P, w], U8, name="q_scales", align_bytes=64)
            nc.vector.quantize_mx(out=q_codes[s][:].bitcast(FP8X4), scales=q_scales[s][:], in_=q_bf[s][:].rearrange("p n j -> p (n j)"))

        def query_matmul(s):
            i, m0, w = QUERY_PARTS[s]
            pair = QUERY_CHUNKS[i][0]
            for a in range(w // P):
                for c in range(2):
                    rows = slice(c * ROWS, (c + 1) * ROWS)
                    nc.tensor.matmul_mx(out=y_bank[c][s % Y_BANKS][:, a, :], lhsT=q_codes[s][rows, a * P:(a + 1) * P].bitcast(FP8X4),
                                        lhsT_scale=q_scales[s][rows, a * P:(a + 1) * P],
                                        rhs=s_codes[pair][rows, :].bitcast(FP8X4), rhs_scale=s_scales[pair][rows, :],
                                        start=True, stop=True)

        def invert(s):
            tiles = QUERY_PARTS[s][2] // P
            for c in range(2):
                inv[(s, c)] = work.tile([P, tiles, 1], F32, name="inv", bufs=2 * len(QUERY_PARTS))
                nc.vector.reciprocal(out=inv[(s, c)][:], in_=y_bank[c][s % Y_BANKS][:, 0:tiles, E - 1:E])

        def finish(s, c, engine):
            i, m0, w = QUERY_PARTS[s]
            pair, n0 = QUERY_CHUNKS[i][0:2]
            tiles = w // P
            bank = y_bank[c][s % Y_BANKS]
            result = work.tile([P, tiles, E], F32, name="result", bufs=RESULT_BUFS)
            if engine == VECTOR:
                nc.vector.tensor_tensor(out=result[:], in0=bank[:, 0:tiles, :], in1=inv[(s, c)][:].to_broadcast([P, tiles, E]), op=ALU.mult)
            else:
                for a in range(tiles):
                    nc.scalar.activation(out=result[:, a, :], in_=bank[:, a, :], func=ACT.Copy, scale=inv[(s, c)][:, a, :])
            nc.sync.dma_start(out=out[2 * pair + c, n0 + m0:n0 + m0 + w, :].rearrange("(a r) e -> r a e", r=P), in_=result[:])

        key_exp(0)
        key_relu(0, VECTOR)
        key_weight(1, SCALAR)
        key_exp(1)
        key_weight(0, VECTOR)
        key_phi(0)
        key_relu(1, VECTOR)
        key_round(0)
        key_relu(2, VECTOR)
        key_exp(2)
        key_phi(1)
        key_phi(2)
        key_round(1)
        key_exp(3)
        key_relu(3, SCALAR)
        key_relu(4, VECTOR)
        key_round(2)
        key_exp(4)
        key_phi(3)
        value_round(0, SCALAR)
        key_quant(0)
        key_phi(4)
        value_quant(0)
        key_round(4)
        value_round(1, VECTOR)
        key_relu(5, SCALAR)
        key_round(3)
        key_exp(5)
        query_weight_abs()
        value_quant(1)
        key_phi(5)
        key_exp(6)
        key_quant(1)
        key_round(5)
        key_relu(6, SCALAR)
        query_weight_sign()
        key_phi(6)
        query_exp(0)
        state_matmul(1)
        value_round(3, VECTOR)
        key_round(6)
        state_matmul(0)
        value_round(2, SCALAR)
        state_evict(0)
        value_quant(3)
        query_exp(1)
        key_quant(2)
        query_exp(3)
        state_park(0)
        query_relu(1)
        state_fetch(0)
        value_quant(2)
        key_quant(3)
        state_matmul(2)
        query_clip(1)
        state_matmul(3)
        state_evict(1)
        query_relu(0)
        state_park(1)
        query_exp(2)
        state_round(0, SCALAR)
        query_relu(2)
        state_fetch(1)
        query_clip(0)
        query_clip(3)
        query_round(1)
        query_round(0)
        state_quant(0)
        query_quant(1)
        query_clip(2)
        query_exp(4)
        query_matmul(1)
        query_quant(0)
        invert(1)
        query_relu(3)
        state_round(1, VECTOR)
        query_round(2)
        query_matmul(0)
        invert(0)
        state_quant(1)
        query_quant(2)
        finish(1, 1, SCALAR)
        finish(1, 0, SCALAR)
        query_round(3)
        finish(0, 0, SCALAR)
        query_clip(4)
        query_matmul(2)
        finish(0, 1, SCALAR)
        query_relu(4)
        invert(2)
        finish(2, 1, SCALAR)
        query_quant(3)
        query_round(5)
        finish(2, 0, SCALAR)
        query_matmul(3)
        query_round(4)
        query_quant(5)
        invert(3)
        finish(3, 0, SCALAR)
        query_matmul(5)
        query_quant(4)
        finish(3, 1, SCALAR)
        query_matmul(4)
        invert(5)
        finish(5, 1, SCALAR)
        invert(4)
        finish(5, 0, SCALAR)
        finish(4, 1, SCALAR)
        finish(4, 0, VECTOR)
